import numpy as np
import ml_dtypes


def mxq(x, axis, fmt="e4m3"):
    dtype, down = {"e4m3": (ml_dtypes.float8_e4m3fn, 7), "e5m2": (ml_dtypes.float8_e5m2, 14)}[fmt]
    v = np.moveaxis(np.asarray(x, np.float32).astype(ml_dtypes.bfloat16).astype(np.float64), axis, -1)
    blocks = v.reshape(v.shape[:-1] + (-1, 32))
    amax = np.abs(blocks).max(-1, keepdims=True)
    byte = np.maximum(np.where(amax > 0, np.frexp(amax)[1] - 1 + 127, 0) - down, 1)
    scale = np.exp2(byte - 127.0)
    codes = (blocks / scale).astype(np.float32).astype(dtype).astype(np.float64)
    return np.moveaxis((codes * scale).reshape(v.shape), -1, axis)


WIDE = False


def mx_kscale(k):
    if not WIDE:
        return np.ones(k)
    levels = np.array([10, -10, 5, -5, 0])
    if k % 512:
        return np.exp2(np.random.permutation(np.resize(levels, k // 32))).repeat(32)
    a = np.empty((k // 512, 16))
    for p in range(k // 512):
        a[p, :8] = np.random.permutation(np.resize(levels, 8))
        for g in range(8):
            far = levels[np.abs(levels - a[p, g]) >= 10]
            a[p, g + 8] = far[np.random.randint(len(far))]
    return np.exp2(a.ravel()).repeat(32)


def f64(x):
    return np.asarray(x).astype(np.float64)


def striped(idx):
    return np.tile(idx.reshape(-1, 16).T, (8, 1)).astype(np.uint16)


def unstriped(offs):
    return offs[:16].T.reshape(-1).astype(np.int64)


def striped8(idx):
    return np.concatenate([x.reshape(-1, 16).T for x in idx]).astype(np.uint16)


def runs(offs, k):
    lists = np.stack([offs[16 * r : 16 * r + 16].T.reshape(-1) for r in range(8)]).astype(np.int64)
    return lists[np.arange(k) % 512 // 64]


def pack_weight(w):
    k, n = w.shape
    w = f64(np.asarray(w, np.float32).astype(ml_dtypes.bfloat16)).reshape(k // 32, 32, n)
    amax = np.abs(w).max(1)
    byte = np.clip(np.where(amax > 0, np.frexp(amax)[1] - 1 + 127 - 7, 1), 1, 254)
    scaled = (w * np.exp2(127.0 - byte)[:, None, :]).reshape(k, n).astype(np.float32)
    words = np.ascontiguousarray(scaled.reshape(k // 512, 128, 4, n).transpose(0, 1, 3, 2)).astype(ml_dtypes.float8_e4m3fn).view(np.uint8)
    return words, np.ascontiguousarray(byte.astype(np.uint8).reshape(k // 512, 16, n))


def unpack_weight(words, scales):
    g, p, n, _ = words.shape
    vals = np.ascontiguousarray(words).view(ml_dtypes.float8_e4m3fn).astype(np.float64) * np.repeat(np.exp2(scales.astype(np.float64) - 127.0), 8, axis=1)[..., None]
    return vals.transpose(0, 1, 3, 2).reshape(g * 512, n)


def relu(v):
    return np.maximum(v, 0.0)

def planes(y):
    n, m = y.shape
    v = y.astype(np.float32).astype(ml_dtypes.bfloat16).astype(np.float64).reshape(n // 32, 32, m)
    top = np.abs(v).max(1)
    byte = np.clip(np.where(top > 0, np.frexp(top)[1] - 1 + 127 - 7, 1), 1, 254)
    codes = (v * np.exp2(127.0 - byte)[:, None, :]).reshape(n, m).astype(np.float32).astype(ml_dtypes.float8_e4m3fn).view(np.uint8)
    words = codes.reshape(n // 512, 128, 4, m).transpose(0, 1, 3, 2)
    return np.ascontiguousarray(words), np.ascontiguousarray(byte.astype(np.uint8).reshape(n // 512, 16, m))


K, T, S, G, H, U = 512, 1024, 512, 2048, 512, 1024


def setup_inputs():
    n = np.random.standard_normal
    s = mx_kscale(K)[:, None]
    packed_xT = pack_weight(n((K, T)) * s)
    packed_dT = pack_weight(n((K, G)) / s)
    return {
        "x_words": packed_xT[0],
        "x_scales": packed_xT[1],
        "d_words": packed_dT[0],
        "d_scales": packed_dT[1],
        "gs": (np.random.uniform(0.5, 1.5, (K, 1)) * s).astype(np.float32),
        "offs": striped(np.random.permutation(T)[:S]),
        "k1": striped8(np.random.randint(0, G, (8, H))),
        "n1": striped8(np.stack([np.random.permutation(U)[:S] for _ in range(8)])),
        "n2": striped8(np.stack([np.random.permutation(S) for _ in range(8)])),
        "k2": striped8(np.random.randint(0, G, (8, H))),
        "n3": striped8(np.stack([np.random.permutation(U) for _ in range(8)])),
        "n4": striped8(np.stack([np.random.permutation(U) for _ in range(8)])),
    }


def reference(x_words, x_scales, d_words, d_scales, gs, offs, k1, n1, n2, k2, n3, n4):
    d_k2 = unpack_weight(d_words, d_scales)[np.arange(K)[:, None], runs(k2, K)]
    d_k1 = unpack_weight(d_words, d_scales)[np.arange(K)[:, None], runs(k1, K)]
    xq = unpack_weight(x_words, x_scales)[:, unstriped(offs)]
    h = 0.0625 * (d_k1.T @ xq)
    nw = h - (relu(h[np.arange(H)[:, None], runs(n2, H)]))
    pg = np.zeros((H, U))
    pg[np.arange(H)[:, None], runs(n1, H)] = nw
    z = f64(gs) * pg
    h2 = 0.0625 * ((d_k2.T @ mxq(z, 0, "e4m3")))
    out_0 = 0.75 * ((h2 - (h2[np.arange(H)[:, None], runs(n3, H)])) * (h2 - (h2[np.arange(H)[:, None], runs(n4, H)])))
    return (out_0,) + planes(out_0)

@@ -1,0 +1,221 @@
+from contextlib import ExitStack
+
+import concourse.mybir as mybir
+
+K, T, S, G, H, U = 512, 1024, 512, 2048, 512, 1024
+FLOPS = 2 * K * H * S + 2 * K * H * U
+
+F32 = mybir.dt.float32
+BF16 = mybir.dt.bfloat16
+I32 = mybir.dt.int32
+U32 = mybir.dt.uint32
+U16 = mybir.dt.uint16
+U8 = mybir.dt.uint8
+FP8X4 = mybir.dt.float8_e4m3fn_x4
+ALU = mybir.AluOpType
+ACT = mybir.ActivationFunctionType
+
+P = 128
+PACK = 4
+QUADS = 4
+BANK = 512
+CHUNKS = ((0, 512), (512, 768), (768, 1024))
+
+
+def tile_picked_codepagezquad_none_po_kernel(
+    tc, x_words, x_scales, d_words, d_scales, gs, offs, k1, n1, n2, k2, n3, n4, out_0, out_1, out_2
+):
+    nc = tc.nc
+    with ExitStack() as ctx:
+        lists = ctx.enter_context(tc.tile_pool(name="lists", bufs=1))
+        keep = ctx.enter_context(tc.tile_pool(name="keep", bufs=1))
+        psum = ctx.enter_context(tc.psum_pool(name="psum", bufs=1))
+
+        def load_list(source, name):
+            tile = lists.tile(list(source.shape), U16, name=name)
+            nc.sync.dma_start(tile[:], source)
+            return tile
+
+        def zeroed_bytes(width, name):
+            tile = keep.tile([P, width], U8, name=name, align_bytes=64)
+            nc.vector.memset(tile[:].bitcast(I32), 0)
+            return tile
+
+        x_scale_table = keep.tile([P, T], U8, align_bytes=64)
+        nc.gpsimd.memset(x_scale_table[:].bitcast(I32), 0)
+        d_scale_table = zeroed_bytes(G, "d_scale_table")
+        offs_list = load_list(offs, "offs_list")
+        k1_list = load_list(k1, "k1_list")
+        nc.scalar.dma_start(x_scale_table[0:P:8, :].bitcast(I32), x_scales[0].bitcast(I32))
+        nc.scalar.dma_start(d_scale_table[0:P:8, :].bitcast(I32), d_scales[0].bitcast(I32))
+        x_word_table = keep.tile([P, T], I32)
+        nc.sync.dma_start(x_word_table[:], x_words[0].rearrange("p n t -> p (n t)").bitcast(I32))
+        d_word_table = keep.tile([P, G], I32)
+        nc.sync.dma_start(d_word_table[:], d_words[0].rearrange("p n t -> p (n t)").bitcast(I32))
+        gs_rows = keep.tile([P, PACK], F32)
+        nc.sync.dma_start(gs_rows[:], gs.rearrange("(p t) one -> p (t one)", t=PACK))
+        n2_list = load_list(n2, "n2_list")
+        n1_list = load_list(n1, "n1_list")
+        k2_list = load_list(k2, "k2_list")
+        n3_list = load_list(n3, "n3_list")
+        n4_list = load_list(n4, "n4_list")
+
+        placed_1 = zeroed_bytes(S + H, "placed_1")
+        placed_2 = zeroed_bytes(H, "placed_2")
+        pages = []
+        for t in range(PACK):
+            page = keep.tile([P, U], F32, name="page%d" % t)
+            nc.vector.memset(page[:], 0.0)
+            pages.append(page)
+
+        minus_gs = keep.tile([P, PACK], F32)
+        nc.scalar.activation(minus_gs[:], gs_rows[:], ACT.Copy, scale=-1.0)
+
+        def place_scale_rows(placed, picked):
+            for q in range(QUADS):
+                queue = nc.sync if q % 2 == 0 else nc.scalar
+                queue.dma_start(
+                    placed[32 * q : 32 * q + 4, :].bitcast(I32),
+                    picked[32 * q : 32 * q + 32 : 8, :].bitcast(I32),
+                )
+
+        def deal(dealt, picked, run):
+            nc.vector.tensor_copy(
+                dealt.rearrange("p (t c i) -> p c t i", t=PACK, i=run),
+                picked.rearrange("p (c i t) -> p c t i", t=PACK, i=run),
+            )
+
+        picked_bytes_1 = keep.tile([P, S + H], U8, tag="picked_bytes", align_bytes=64)
+        nc.vector.tensor_copy(picked_bytes_1[:, 0:S], x_scale_table[:].indirect(offs_list[:]))
+        nc.vector.tensor_copy(picked_bytes_1[:, S : S + H], d_scale_table[:].indirect(k1_list[:]))
+        place_scale_rows(placed_1, picked_bytes_1)
+        x_codes = keep.tile([P, S], U32, align_bytes=64)
+        nc.vector.tensor_copy(x_codes[:], x_word_table[:].bitcast(U32).indirect(offs_list[:]))
+        picked_words_1 = keep.tile([P, H], U32, align_bytes=64)
+        nc.vector.tensor_copy(picked_words_1[:], d_word_table[:].bitcast(U32).indirect(k1_list[:]))
+        w1_codes = keep.tile([P, H], U32, align_bytes=64)
+        deal(w1_codes[:], picked_words_1[:], 4)
+        w1_scales = keep.tile([P, H], U8, align_bytes=64)
+        deal(w1_scales[:], placed_1[:, S : S + H], 16)
+
+        h_tiles = []
+        for t in range(PACK):
+            bank = psum.tile([P, BANK], F32, name="h_bank", tag="bank%d" % (2 * t + 1))
+            rows = slice(t * P, (t + 1) * P)
+            nc.tensor.matmul_mx(
+                bank[:],
+                lhsT=w1_codes[:, rows].bitcast(FP8X4),
+                lhsT_scale=w1_scales[:, rows],
+                rhs=x_codes[:].bitcast(FP8X4),
+                rhs_scale=placed_1[:, 0:S],
+                start=True,
+                stop=True,
+            )
+            h_tile = keep.tile([P, 2 * S], F32, name="h%d" % t)
+            nc.scalar.activation(h_tile[:, 0:S], bank[:], ACT.Relu, scale=0.0625)
+            nc.scalar.activation(h_tile[:, S : 2 * S], bank[:], ACT.Copy, scale=-0.0625)
+            h_tiles.append(h_tile)
+
+        picked_bytes_2 = keep.tile([P, H], U8, tag="picked_bytes", align_bytes=64)
+        nc.vector.tensor_copy(picked_bytes_2[:], d_scale_table[:].indirect(k2_list[:]))
+        place_scale_rows(placed_2, picked_bytes_2)
+
+        z_tiles = [
+            keep.tile([P, hi - lo, PACK], BF16, name="z%d" % c, align_bytes=64) for c, (lo, hi) in enumerate(CHUNKS)
+        ]
+        fetched = []
+
+        def fetch(t):
+            tile = keep.tile([P, S], F32, name="fetched", tag="fetched%d" % t, align_bytes=64)
+            nc.vector.tensor_copy(tile[:], h_tiles[t][:].indirect(n2_list[:]))
+            fetched.append(tile)
+
+        fetch(0)
+        for t in range(PACK):
+            if t + 1 < PACK:
+                fetch(t + 1)
+            nc.vector.tensor_tensor(
+                pages[t][:].indirect(n1_list[:]), fetched[t][:], h_tiles[t][:, S : 2 * S], ALU.add
+            )
+            for c, (lo, hi) in enumerate(CHUNKS):
+                nc.scalar.activation(z_tiles[c][:, :, t], pages[t][:, lo:hi], ACT.Copy, scale=minus_gs[:, t : t + 1])
+
+        w2_scales = keep.tile([P, H], U8, align_bytes=64)
+        deal(w2_scales[:], placed_2[:], 16)
+        picked_words_2 = keep.tile([P, H], U32, tag="fetched%d" % (PACK - 1), align_bytes=64)
+        nc.vector.tensor_copy(picked_words_2[:], d_word_table[:].bitcast(U32).indirect(k2_list[:]))
+        w2_codes = keep.tile([P, H], U32, align_bytes=64)
+        deal(w2_codes[:], picked_words_2[:], 4)
+
+        z_codes, z_scales = [], []
+        z_scale_plane = zeroed_bytes(U, "z_scale_plane")
+        for c, (lo, hi) in enumerate(CHUNKS):
+            codes = keep.tile([P, hi - lo], U32, name="z_codes%d" % c, align_bytes=64)
+            scales = z_scale_plane[:, lo:hi]
+            nc.vector.quantize_mx(codes[:].bitcast(FP8X4), scales, z_tiles[c][:].rearrange("p w t -> p (w t)"))
+            z_codes.append(codes)
+            z_scales.append(scales)
+
+        h2_tiles, h2_twins, h2_banks = [], [], []
+        for t in range(PACK):
+            banks = [psum.tile([P, BANK], F32, name="h2_bank", tag="bank%d" % (2 * t + b)) for b in range(2)]
+            rows = slice(t * P, (t + 1) * P)
+            for c, (lo, hi) in enumerate(CHUNKS):
+                b = lo // BANK
+                nc.tensor.matmul_mx(
+                    banks[b][:, lo - b * BANK : hi - b * BANK],
+                    lhsT=w2_codes[:, rows].bitcast(FP8X4),
+                    lhsT_scale=w2_scales[:, rows],
+                    rhs=z_codes[c][:].bitcast(FP8X4),
+                    rhs_scale=z_scales[c],
+                    start=True,
+                    stop=True,
+                )
+            h2 = keep.tile([P, U], F32, name="h2_%d" % t)
+            twin = keep.tile([P, U], F32, name="h2_twin%d" % t)
+            nc.scalar.activation(h2[:, 0:BANK], banks[0][:], ACT.Copy, scale=0.0625)
+            nc.scalar.activation(twin[:, 0:BANK], banks[0][:], ACT.Copy, scale=0.0625)
+            nc.scalar.activation(h2[:, BANK:U], banks[1][:], ACT.Copy, scale=0.0625)
+            h2_tiles.append(h2)
+            h2_twins.append(twin)
+            h2_banks.append(banks)
+        for t in range(PACK):
+            nc.scalar.activation(h2_twins[t][:, BANK:U], h2_banks[t][1][:], ACT.Copy, scale=0.0625)
+
+        out_rows = out_0.rearrange("(p t) w -> p t w", t=PACK)
+        out_words = out_1[0].rearrange("p n t -> p (n t)").bitcast(I32)
+        out_scales = keep.tile([P, U], U8, align_bytes=64)
+        for c, (lo, hi) in enumerate(CHUNKS):
+            width = hi - lo
+            entries = slice(lo // 16, hi // 16)
+            diff_3 = keep.tile([P, PACK, width], F32, name="diff_3_%d" % c)
+            diff_4 = keep.tile([P, PACK, width], F32, name="diff_4_%d" % c)
+            result = keep.tile([P, PACK, width], F32, name="result%d" % c)
+
+            def multiply(first, last):
+                views = [tile[:, first:last, :].rearrange("p t w -> p (t w)") for tile in (result, diff_3, diff_4)]
+                nc.vector.scalar_tensor_tensor(views[0], views[1], 0.75, views[2], ALU.mult, ALU.mult)
+
+            for t in range(PACK):
+                nc.vector.tensor_tensor(
+                    diff_3[:, t, :], h2_tiles[t][:].indirect(n3_list[:, entries]), h2_twins[t][:, lo:hi], ALU.subtract
+                )
+                if t == PACK - 1:
+                    multiply(0, t)
+                nc.vector.tensor_tensor(
+                    diff_4[:, t, :], h2_tiles[t][:].indirect(n4_list[:, entries]), h2_twins[t][:, lo:hi], ALU.subtract
+                )
+            multiply(PACK - 1, PACK)
+            nc.sync.dma_start(out_rows[:, :, lo:hi], result[:])
+            rounded = keep.tile([P, width, PACK], BF16, name="rounded%d" % c, align_bytes=64)
+            nc.scalar.activation(
+                rounded[:].rearrange("p (c i) t -> p c t i", i=4),
+                result[:].rearrange("p t (c i) -> p c t i", i=4),
+                ACT.Copy,
+            )
+            codes = keep.tile([P, width], I32, name="out_codes%d" % c, align_bytes=64)
+            nc.vector.quantize_mx(codes[:].bitcast(FP8X4), out_scales[:, lo:hi], rounded[:].rearrange("p w t -> p (w t)"))
+            nc.sync.dma_start(out_words[:, lo:hi], codes[:])
+        for q in range(QUADS):
+            queue = nc.scalar if q % 2 == 0 else nc.sync
+            queue.dma_start(out_2[0, 4 * q : 4 * q + 4, :].bitcast(I32), out_scales[32 * q : 32 * q + 4, :].bitcast(I32))

@@ -41,26 +41,28 @@ def tile_picked_codepagezquad_none_po_kernel(
             nc.vector.memset(tile[:].bitcast(I32), 0)
             return tile
 
-        x_scale_table = keep.tile([P, T], U8, align_bytes=64)
-        nc.gpsimd.memset(x_scale_table[:].bitcast(I32), 0)
-        d_scale_table = zeroed_bytes(G, "d_scale_table")
+        d_scale_table = keep.tile([P, G], U8, align_bytes=64)
+        nc.gpsimd.memset(d_scale_table[:].bitcast(I32), 0)
+        x_scale_table = keep.tile([P, T], U8, tag="x_scales_then_words", align_bytes=64)
+        nc.vector.memset(x_scale_table[:].bitcast(I32), 0)
+        nc.scalar.dma_start(d_scale_table[0:P:8, :].bitcast(I32), d_scales[0].bitcast(I32))
+        nc.scalar.dma_start(x_scale_table[0:P:8, :].bitcast(I32), x_scales[0].bitcast(I32))
         offs_list = load_list(offs, "offs_list")
         k1_list = load_list(k1, "k1_list")
-        nc.scalar.dma_start(x_scale_table[0:P:8, :].bitcast(I32), x_scales[0].bitcast(I32))
-        nc.scalar.dma_start(d_scale_table[0:P:8, :].bitcast(I32), d_scales[0].bitcast(I32))
+        n2_list = load_list(n2, "n2_list")
+        n1_list = load_list(n1, "n1_list")
         x_word_table = keep.tile([P, T], I32)
         nc.sync.dma_start(x_word_table[:], x_words[0].rearrange("p n t -> p (n t)").bitcast(I32))
         d_word_table = keep.tile([P, G], I32)
         nc.sync.dma_start(d_word_table[:], d_words[0].rearrange("p n t -> p (n t)").bitcast(I32))
-        gs_rows = keep.tile([P, PACK], F32)
-        nc.sync.dma_start(gs_rows[:], gs.rearrange("(p t) one -> p (t one)", t=PACK))
-        n2_list = load_list(n2, "n2_list")
-        n1_list = load_list(n1, "n1_list")
         k2_list = load_list(k2, "k2_list")
         n3_list = load_list(n3, "n3_list")
         n4_list = load_list(n4, "n4_list")
+        gs_rows = keep.tile([P, PACK], F32)
+        nc.sync.dma_start(gs_rows[:], gs.rearrange("(p t) one -> p (t one)", t=PACK))
 
-        placed_1 = zeroed_bytes(S + H, "placed_1")
+        placed_1 = zeroed_bytes(H, "placed_1")
+        x_scale_plane = zeroed_bytes(S, "x_scale_plane")
         placed_2 = zeroed_bytes(H, "placed_2")
         pages = []
         for t in range(PACK):
@@ -68,8 +70,6 @@ def tile_picked_codepagezquad_none_po_kernel(
             nc.vector.memset(page[:], 0.0)
             pages.append(page)
 
-        minus_gs = keep.tile([P, PACK], F32)
-        nc.scalar.activation(minus_gs[:], gs_rows[:], ACT.Copy, scale=-1.0)
 
         def place_scale_rows(placed, picked):
             for q in range(QUADS):
@@ -79,42 +79,48 @@ def tile_picked_codepagezquad_none_po_kernel(
                     picked[32 * q : 32 * q + 32 : 8, :].bitcast(I32),
                 )
 
-        def deal(dealt, picked, run):
+        def deal(dealt, picked, run, first=0, last=PACK):
             nc.vector.tensor_copy(
-                dealt.rearrange("p (t c i) -> p c t i", t=PACK, i=run),
-                picked.rearrange("p (c i t) -> p c t i", t=PACK, i=run),
+                dealt.rearrange("p (t c i) -> p c t i", t=last - first, i=run),
+                picked.rearrange("p (c i t) -> p c t i", t=PACK, i=run)[:, :, first:last, :],
             )
 
-        picked_bytes_1 = keep.tile([P, S + H], U8, tag="picked_bytes", align_bytes=64)
-        nc.vector.tensor_copy(picked_bytes_1[:, 0:S], x_scale_table[:].indirect(offs_list[:]))
-        nc.vector.tensor_copy(picked_bytes_1[:, S : S + H], d_scale_table[:].indirect(k1_list[:]))
+        picked_bytes_1 = keep.tile([P, H], U8, align_bytes=64)
+        nc.vector.tensor_copy(picked_bytes_1[:], d_scale_table[:].indirect(k1_list[:]))
         place_scale_rows(placed_1, picked_bytes_1)
+        picked_bytes_x = keep.tile([P, S], U8, tag="picked_bytes", align_bytes=64)
+        nc.vector.tensor_copy(picked_bytes_x[:], x_scale_table[:].indirect(offs_list[:]))
+        place_scale_rows(x_scale_plane, picked_bytes_x)
         x_codes = keep.tile([P, S], U32, align_bytes=64)
         nc.vector.tensor_copy(x_codes[:], x_word_table[:].bitcast(U32).indirect(offs_list[:]))
-        picked_words_1 = keep.tile([P, H], U32, align_bytes=64)
+        picked_words_1 = keep.tile([P, H], U32, tag="x_scales_then_words", align_bytes=64)
         nc.vector.tensor_copy(picked_words_1[:], d_word_table[:].bitcast(U32).indirect(k1_list[:]))
-        w1_codes = keep.tile([P, H], U32, align_bytes=64)
-        deal(w1_codes[:], picked_words_1[:], 4)
+        w1_first = keep.tile([P, P], U32, align_bytes=64)
+        deal(w1_first[:], picked_words_1[:], 4, 0, 1)
         w1_scales = keep.tile([P, H], U8, align_bytes=64)
-        deal(w1_scales[:], placed_1[:, S : S + H], 16)
+        deal(w1_scales[:], placed_1[:], 16)
+        w1_rest = keep.tile([P, H - P], U32, tag="placed_1", align_bytes=64)
+        deal(w1_rest[:], picked_words_1[:], 4, 1, PACK)
+        w1_codes = [w1_first[:]] + [w1_rest[:, t * P : (t + 1) * P] for t in range(PACK - 1)]
 
-        h_tiles = []
+        h_tiles = [keep.tile([P, 2 * S], F32, name="h%d" % t) for t in range(PACK)]
+        nc.vector.memset(h_tiles[0][:, S : 2 * S], 0.0)
+        last_minus_h = keep.tile([P, S], F32)
+        minus_h = [h_tiles[t + 1][:, S : 2 * S] for t in range(PACK - 1)] + [last_minus_h[:]]
         for t in range(PACK):
             bank = psum.tile([P, BANK], F32, name="h_bank", tag="bank%d" % (2 * t + 1))
             rows = slice(t * P, (t + 1) * P)
             nc.tensor.matmul_mx(
                 bank[:],
-                lhsT=w1_codes[:, rows].bitcast(FP8X4),
+                lhsT=w1_codes[t].bitcast(FP8X4),
                 lhsT_scale=w1_scales[:, rows],
                 rhs=x_codes[:].bitcast(FP8X4),
-                rhs_scale=placed_1[:, 0:S],
+                rhs_scale=x_scale_plane[:],
                 start=True,
                 stop=True,
             )
-            h_tile = keep.tile([P, 2 * S], F32, name="h%d" % t)
-            nc.scalar.activation(h_tile[:, 0:S], bank[:], ACT.Relu, scale=0.0625)
-            nc.scalar.activation(h_tile[:, S : 2 * S], bank[:], ACT.Copy, scale=-0.0625)
-            h_tiles.append(h_tile)
+            nc.scalar.activation(h_tiles[t][:, 0:S], bank[:], ACT.Relu, scale=0.0625)
+            nc.scalar.activation(minus_h[t], bank[:], ACT.Copy, scale=-0.0625)
 
         picked_bytes_2 = keep.tile([P, H], U8, tag="picked_bytes", align_bytes=64)
         nc.vector.tensor_copy(picked_bytes_2[:], d_scale_table[:].indirect(k2_list[:]))
@@ -124,6 +130,7 @@ def tile_picked_codepagezquad_none_po_kernel(
             keep.tile([P, hi - lo, PACK], BF16, name="z%d" % c, align_bytes=64) for c, (lo, hi) in enumerate(CHUNKS)
         ]
         fetched = []
+        w2_scales = keep.tile([P, H], U8, align_bytes=64)
 
         def fetch(t):
             tile = keep.tile([P, S], F32, name="fetched", tag="fetched%d" % t, align_bytes=64)
@@ -135,36 +142,50 @@ def tile_picked_codepagezquad_none_po_kernel(
             if t + 1 < PACK:
                 fetch(t + 1)
             nc.vector.tensor_tensor(
-                pages[t][:].indirect(n1_list[:]), fetched[t][:], h_tiles[t][:, S : 2 * S], ALU.add
+                pages[t][:].indirect(n1_list[:]), fetched[t][:], minus_h[t], ALU.add
             )
+            if t == 0:
+                deal(w2_scales[:], placed_2[:], 16)
+            minus_gs = keep.tile([P, 1], F32)
+            nc.scalar.activation(minus_gs[:], gs_rows[:, t : t + 1], ACT.Copy, scale=-1.0)
             for c, (lo, hi) in enumerate(CHUNKS):
-                nc.scalar.activation(z_tiles[c][:, :, t], pages[t][:, lo:hi], ACT.Copy, scale=minus_gs[:, t : t + 1])
+                if (t, c) != (PACK - 1, len(CHUNKS) - 1):
+                    nc.scalar.activation(
+                        z_tiles[c][:, :, t], pages[t][:, lo:hi], ACT.Copy, scale=minus_gs[:]
+                    )
 
-        w2_scales = keep.tile([P, H], U8, align_bytes=64)
-        deal(w2_scales[:], placed_2[:], 16)
         picked_words_2 = keep.tile([P, H], U32, tag="fetched%d" % (PACK - 1), align_bytes=64)
         nc.vector.tensor_copy(picked_words_2[:], d_word_table[:].bitcast(U32).indirect(k2_list[:]))
-        w2_codes = keep.tile([P, H], U32, align_bytes=64)
-        deal(w2_codes[:], picked_words_2[:], 4)
+        w2_first = keep.tile([P, P], U32, align_bytes=64)
+        deal(w2_first[:], picked_words_2[:], 4, 0, 1)
+        lo, hi = CHUNKS[-1]
+        nc.vector.tensor_scalar(
+            z_tiles[-1][:, :, PACK - 1], pages[PACK - 1][:, lo:hi], minus_gs[:], None, ALU.mult
+        )
 
-        z_codes, z_scales = [], []
+        z_codes, z_scales = {}, {}
         z_scale_plane = zeroed_bytes(U, "z_scale_plane")
-        for c, (lo, hi) in enumerate(CHUNKS):
+        for c in (0, 2, 1):
+            lo, hi = CHUNKS[c]
             codes = keep.tile([P, hi - lo], U32, name="z_codes%d" % c, align_bytes=64)
             scales = z_scale_plane[:, lo:hi]
             nc.vector.quantize_mx(codes[:].bitcast(FP8X4), scales, z_tiles[c][:].rearrange("p w t -> p (w t)"))
-            z_codes.append(codes)
-            z_scales.append(scales)
+            z_codes.setdefault(c, codes)
+            z_scales.setdefault(c, scales)
+        w2_rest = keep.tile([P, H - P], U32, tag="z1", align_bytes=64)
+        deal(w2_rest[:], picked_words_2[:], 4, 1, PACK)
+        w2_codes = [w2_first[:]] + [w2_rest[:, t * P : (t + 1) * P] for t in range(PACK - 1)]
 
         h2_tiles, h2_twins, h2_banks = [], [], []
         for t in range(PACK):
             banks = [psum.tile([P, BANK], F32, name="h2_bank", tag="bank%d" % (2 * t + b)) for b in range(2)]
             rows = slice(t * P, (t + 1) * P)
-            for c, (lo, hi) in enumerate(CHUNKS):
+            for c in (0, 2, 1):
+                lo, hi = CHUNKS[c]
                 b = lo // BANK
                 nc.tensor.matmul_mx(
                     banks[b][:, lo - b * BANK : hi - b * BANK],
-                    lhsT=w2_codes[:, rows].bitcast(FP8X4),
+                    lhsT=w2_codes[t].bitcast(FP8X4),
                     lhsT_scale=w2_scales[:, rows],
                     rhs=z_codes[c][:].bitcast(FP8X4),
                     rhs_scale=z_scales[c],
@@ -175,7 +196,10 @@ def tile_picked_codepagezquad_none_po_kernel(
             twin = keep.tile([P, U], F32, name="h2_twin%d" % t)
             nc.scalar.activation(h2[:, 0:BANK], banks[0][:], ACT.Copy, scale=0.0625)
             nc.scalar.activation(twin[:, 0:BANK], banks[0][:], ACT.Copy, scale=0.0625)
-            nc.scalar.activation(h2[:, BANK:U], banks[1][:], ACT.Copy, scale=0.0625)
+            if t == 0:
+                nc.vector.tensor_scalar(h2[:, BANK:U], banks[1][:], 0.0625, None, ALU.mult)
+            else:
+                nc.scalar.activation(h2[:, BANK:U], banks[1][:], ACT.Copy, scale=0.0625)
             h2_tiles.append(h2)
             h2_twins.append(twin)
             h2_banks.append(banks)
@@ -185,37 +209,61 @@ def tile_picked_codepagezquad_none_po_kernel(
         out_rows = out_0.rearrange("(p t) w -> p t w", t=PACK)
         out_words = out_1[0].rearrange("p n t -> p (n t)").bitcast(I32)
         out_scales = keep.tile([P, U], U8, align_bytes=64)
-        for c, (lo, hi) in enumerate(CHUNKS):
-            width = hi - lo
-            entries = slice(lo // 16, hi // 16)
-            diff_3 = keep.tile([P, PACK, width], F32, name="diff_3_%d" % c)
-            diff_4 = keep.tile([P, PACK, width], F32, name="diff_4_%d" % c)
-            result = keep.tile([P, PACK, width], F32, name="result%d" % c)
+        diff_3 = keep.tile([P, 2, PACK, BANK], F32)
+        diff_4 = keep.tile([P, 2, PACK, BANK], F32)
+        result = keep.tile([P, 2, PACK, BANK], F32)
+        rounded = keep.tile([P, U, PACK], BF16, align_bytes=64)
+        out_codes = keep.tile([P, U], I32, align_bytes=64)
 
-            def multiply(first, last):
-                views = [tile[:, first:last, :].rearrange("p t w -> p (t w)") for tile in (result, diff_3, diff_4)]
-                nc.vector.scalar_tensor_tensor(views[0], views[1], 0.75, views[2], ALU.mult, ALU.mult)
+        def differ(diff, index_list, t, lo, hi):
+            nc.vector.tensor_tensor(
+                diff[:, lo // BANK, t, lo % BANK : lo % BANK + hi - lo],
+                h2_tiles[t][:].indirect(index_list[:, lo // 16 : hi // 16]),
+                h2_twins[t][:, lo:hi],
+                ALU.subtract,
+            )
 
-            for t in range(PACK):
-                nc.vector.tensor_tensor(
-                    diff_3[:, t, :], h2_tiles[t][:].indirect(n3_list[:, entries]), h2_twins[t][:, lo:hi], ALU.subtract
-                )
-                if t == PACK - 1:
-                    multiply(0, t)
-                nc.vector.tensor_tensor(
-                    diff_4[:, t, :], h2_tiles[t][:].indirect(n4_list[:, entries]), h2_twins[t][:, lo:hi], ALU.subtract
-                )
-            multiply(PACK - 1, PACK)
-            nc.sync.dma_start(out_rows[:, :, lo:hi], result[:])
-            rounded = keep.tile([P, width, PACK], BF16, name="rounded%d" % c, align_bytes=64)
+        def finish(first, last, lo, hi):
+            views = [
+                tile[:, lo // BANK, first:last, lo % BANK : lo % BANK + hi - lo] for tile in (result, diff_3, diff_4)
+            ]
+            nc.vector.scalar_tensor_tensor(views[0], views[1], 0.75, views[2], ALU.mult, ALU.mult)
+            nc.sync.dma_start(out_rows[:, first:last, lo:hi], views[0])
             nc.scalar.activation(
-                rounded[:].rearrange("p (c i) t -> p c t i", i=4),
-                result[:].rearrange("p t (c i) -> p c t i", i=4),
+                rounded[:, lo:hi, first:last].rearrange("p (c i) t -> p c t i", i=4),
+                views[0].rearrange("p t (c i) -> p c t i", i=4),
                 ACT.Copy,
             )
-            codes = keep.tile([P, width], I32, name="out_codes%d" % c, align_bytes=64)
-            nc.vector.quantize_mx(codes[:].bitcast(FP8X4), out_scales[:, lo:hi], rounded[:].rearrange("p w t -> p (w t)"))
-            nc.sync.dma_start(out_words[:, lo:hi], codes[:])
+
+        def quantise(lo, hi):
+            nc.vector.quantize_mx(
+                out_codes[:, lo:hi].bitcast(FP8X4),
+                out_scales[:, lo:hi],
+                rounded[:, lo:hi, :].rearrange("p w t -> p (w t)"),
+            )
+            nc.sync.dma_start(out_words[:, lo:hi], out_codes[:, lo:hi])
+
+        last = PACK - 1
+        mid = BANK + BANK // 2
+        for t in range(PACK):
+            differ(diff_3, n3_list, t, 0, BANK)
+            differ(diff_4, n4_list, t, 0, BANK)
+        differ(diff_3, n3_list, 0, BANK, U)
+        finish(0, PACK, 0, BANK)
+        differ(diff_4, n4_list, 0, BANK, U)
+        for t in range(1, last):
+            differ(diff_3, n3_list, t, BANK, U)
+            differ(diff_4, n4_list, t, BANK, U)
+        quantise(0, BANK)
+        differ(diff_3, n3_list, last, BANK, mid)
+        finish(0, last, BANK, U)
+        differ(diff_4, n4_list, last, BANK, mid)
+        differ(diff_3, n3_list, last, mid, U)
+        finish(last, PACK, BANK, mid)
+        differ(diff_4, n4_list, last, mid, U)
+        finish(last, PACK, mid, U)
+        quantise(BANK, mid)
+        quantise(mid, U)
         for q in range(QUADS):
             queue = nc.scalar if q % 2 == 0 else nc.sync
             queue.dma_start(out_2[0, 4 * q : 4 * q + 4, :].bitcast(I32), out_scales[32 * q : 32 * q + 4, :].bitcast(I32))

@@ -38,36 +38,37 @@ def tile_picked_codepagezquad_none_po_kernel(
 
         def zeroed_bytes(width, name):
             tile = keep.tile([P, width], U8, name=name, align_bytes=64)
-            nc.vector.memset(tile[:].bitcast(I32), 0)
+            nc.gpsimd.memset(tile[:].bitcast(I32), 0)
             return tile
 
-        d_scale_table = keep.tile([P, G], U8, align_bytes=64)
-        nc.gpsimd.memset(d_scale_table[:].bitcast(I32), 0)
-        x_scale_table = keep.tile([P, T], U8, tag="x_scales_then_words", align_bytes=64)
-        nc.vector.memset(x_scale_table[:].bitcast(I32), 0)
-        nc.scalar.dma_start(d_scale_table[0:P:8, :].bitcast(I32), d_scales[0].bitcast(I32))
-        nc.scalar.dma_start(x_scale_table[0:P:8, :].bitcast(I32), x_scales[0].bitcast(I32))
-        offs_list = load_list(offs, "offs_list")
+        def load_scale_rows(table, scales):
+            rows = scales[0].bitcast(I32)
+            nc.sync.dma_start(table[:].bitcast(I32), rows.unsqueeze(1).to_broadcast([16, 8, rows.shape[1]]))
+
         k1_list = load_list(k1, "k1_list")
+        d_scale_table = keep.tile([P, G], U8, align_bytes=64)
+        load_scale_rows(d_scale_table, d_scales)
+        offs_list = load_list(offs, "offs_list")
+        x_scale_table = keep.tile([P, T], U8, tag="x_scales_then_words", align_bytes=64)
+        load_scale_rows(x_scale_table, x_scales)
+        x_word_table = keep.tile([P, T], I32)
+        nc.scalar.dma_start(x_word_table[:], x_words[0].rearrange("p n t -> p (n t)").bitcast(I32))
+        d_word_table = keep.tile([P, G], I32)
+        nc.scalar.dma_start(d_word_table[:], d_words[0].rearrange("p n t -> p (n t)").bitcast(I32))
         n2_list = load_list(n2, "n2_list")
         n1_list = load_list(n1, "n1_list")
-        x_word_table = keep.tile([P, T], I32)
-        nc.sync.dma_start(x_word_table[:], x_words[0].rearrange("p n t -> p (n t)").bitcast(I32))
-        d_word_table = keep.tile([P, G], I32)
-        nc.sync.dma_start(d_word_table[:], d_words[0].rearrange("p n t -> p (n t)").bitcast(I32))
         k2_list = load_list(k2, "k2_list")
         n3_list = load_list(n3, "n3_list")
         n4_list = load_list(n4, "n4_list")
         gs_rows = keep.tile([P, PACK], F32)
         nc.sync.dma_start(gs_rows[:], gs.rearrange("(p t) one -> p (t one)", t=PACK))
 
-        placed_1 = zeroed_bytes(H, "placed_1")
-        x_scale_plane = zeroed_bytes(S, "x_scale_plane")
+        placed_1 = zeroed_bytes(S + H, "placed_1")
         placed_2 = zeroed_bytes(H, "placed_2")
         pages = []
         for t in range(PACK):
             page = keep.tile([P, U], F32, name="page%d" % t)
-            nc.vector.memset(page[:], 0.0)
+            nc.gpsimd.memset(page[:], 0.0)
             pages.append(page)
 
 
@@ -85,26 +86,23 @@ def tile_picked_codepagezquad_none_po_kernel(
                 picked.rearrange("p (c i t) -> p c t i", t=PACK, i=run)[:, :, first:last, :],
             )
 
-        picked_bytes_1 = keep.tile([P, H], U8, align_bytes=64)
-        nc.vector.tensor_copy(picked_bytes_1[:], d_scale_table[:].indirect(k1_list[:]))
+        picked_bytes_1 = keep.tile([P, S + H], U8, tag="picked_bytes", align_bytes=64)
+        nc.vector.tensor_copy(picked_bytes_1[:, S : S + H], d_scale_table[:].indirect(k1_list[:]))
+        nc.vector.tensor_copy(picked_bytes_1[:, 0:S], x_scale_table[:].indirect(offs_list[:]))
         place_scale_rows(placed_1, picked_bytes_1)
-        picked_bytes_x = keep.tile([P, S], U8, tag="picked_bytes", align_bytes=64)
-        nc.vector.tensor_copy(picked_bytes_x[:], x_scale_table[:].indirect(offs_list[:]))
-        place_scale_rows(x_scale_plane, picked_bytes_x)
-        x_codes = keep.tile([P, S], U32, align_bytes=64)
-        nc.vector.tensor_copy(x_codes[:], x_word_table[:].bitcast(U32).indirect(offs_list[:]))
-        picked_words_1 = keep.tile([P, H], U32, tag="x_scales_then_words", align_bytes=64)
-        nc.vector.tensor_copy(picked_words_1[:], d_word_table[:].bitcast(U32).indirect(k1_list[:]))
+        picked_words_1 = keep.tile([P, S + H], U32, tag="x_scales_then_words", align_bytes=64)
+        nc.vector.tensor_copy(picked_words_1[:, 0:S], x_word_table[:].bitcast(U32).indirect(offs_list[:]))
+        nc.vector.tensor_copy(picked_words_1[:, S : S + H], d_word_table[:].bitcast(U32).indirect(k1_list[:]))
         w1_first = keep.tile([P, P], U32, align_bytes=64)
-        deal(w1_first[:], picked_words_1[:], 4, 0, 1)
+        deal(w1_first[:], picked_words_1[:, S : S + H], 4, 0, 1)
         w1_scales = keep.tile([P, H], U8, align_bytes=64)
-        deal(w1_scales[:], placed_1[:], 16)
-        w1_rest = keep.tile([P, H - P], U32, tag="placed_1", align_bytes=64)
-        deal(w1_rest[:], picked_words_1[:], 4, 1, PACK)
+        deal(w1_scales[:], placed_1[:, S : S + H], 16)
+        w1_rest = keep.tile([P, H - P], U32, align_bytes=64)
+        deal(w1_rest[:], picked_words_1[:, S : S + H], 4, 1, PACK)
         w1_codes = [w1_first[:]] + [w1_rest[:, t * P : (t + 1) * P] for t in range(PACK - 1)]
 
         h_tiles = [keep.tile([P, 2 * S], F32, name="h%d" % t) for t in range(PACK)]
-        nc.vector.memset(h_tiles[0][:, S : 2 * S], 0.0)
+        nc.gpsimd.memset(h_tiles[0][:, S : 2 * S], 0.0)
         last_minus_h = keep.tile([P, S], F32)
         minus_h = [h_tiles[t + 1][:, S : 2 * S] for t in range(PACK - 1)] + [last_minus_h[:]]
         for t in range(PACK):
@@ -114,8 +112,8 @@ def tile_picked_codepagezquad_none_po_kernel(
                 bank[:],
                 lhsT=w1_codes[t].bitcast(FP8X4),
                 lhsT_scale=w1_scales[:, rows],
-                rhs=x_codes[:].bitcast(FP8X4),
-                rhs_scale=x_scale_plane[:],
+                rhs=picked_words_1[:, 0:S].bitcast(FP8X4),
+                rhs_scale=placed_1[:, 0:S],
                 start=True,
                 stop=True,
             )

@@ -19,7 +19,7 @@ P = 128
 PACK = 4
 QUADS = 4
 BANK = 512
-CHUNKS = ((0, 512), (512, 768), (768, 1024))
+CHUNKS = ((0, 256), (256, 512), (512, 768), (768, 1024))
 
 
 def tile_picked_codepagezquad_none_po_kernel(
@@ -38,7 +38,7 @@ def tile_picked_codepagezquad_none_po_kernel(
 
         def zeroed_bytes(width, name):
             tile = keep.tile([P, width], U8, name=name, align_bytes=64)
-            nc.gpsimd.memset(tile[:].bitcast(I32), 0)
+            nc.vector.memset(tile[:].bitcast(I32), 0)
             return tile
 
         def load_scale_rows(table, scales):
@@ -52,23 +52,22 @@ def tile_picked_codepagezquad_none_po_kernel(
         x_scale_table = keep.tile([P, T], U8, tag="x_scales_then_words", align_bytes=64)
         load_scale_rows(x_scale_table, x_scales)
         x_word_table = keep.tile([P, T], I32)
-        nc.scalar.dma_start(x_word_table[:], x_words[0].rearrange("p n t -> p (n t)").bitcast(I32))
-        d_word_table = keep.tile([P, G], I32)
-        nc.scalar.dma_start(d_word_table[:], d_words[0].rearrange("p n t -> p (n t)").bitcast(I32))
+        nc.sync.dma_start(x_word_table[:], x_words[0].rearrange("p n t -> p (n t)").bitcast(I32))
         n2_list = load_list(n2, "n2_list")
         n1_list = load_list(n1, "n1_list")
         k2_list = load_list(k2, "k2_list")
+        d_word_table = keep.tile([P, G], I32)
+        nc.sync.dma_start(d_word_table[:], d_words[0].rearrange("p n t -> p (n t)").bitcast(I32))
         n3_list = load_list(n3, "n3_list")
         n4_list = load_list(n4, "n4_list")
         gs_rows = keep.tile([P, PACK], F32)
         nc.sync.dma_start(gs_rows[:], gs.rearrange("(p t) one -> p (t one)", t=PACK))
 
         placed_1 = zeroed_bytes(S + H, "placed_1")
-        placed_2 = zeroed_bytes(H, "placed_2")
         pages = []
-        for t in range(PACK):
+        for t in range(2):
             page = keep.tile([P, U], F32, name="page%d" % t)
-            nc.gpsimd.memset(page[:], 0.0)
+            (nc.vector if t == 0 else nc.gpsimd).memset(page[:], 0.0)
             pages.append(page)
 
 
@@ -101,8 +100,7 @@ def tile_picked_codepagezquad_none_po_kernel(
         deal(w1_rest[:], picked_words_1[:, S : S + H], 4, 1, PACK)
         w1_codes = [w1_first[:]] + [w1_rest[:, t * P : (t + 1) * P] for t in range(PACK - 1)]
 
-        h_tiles = [keep.tile([P, 2 * S], F32, name="h%d" % t) for t in range(PACK)]
-        nc.gpsimd.memset(h_tiles[0][:, S : 2 * S], 0.0)
+        h_tiles = [keep.tile([P, 2 * S if t > 0 else S], F32, name="h%d" % t) for t in range(PACK)]
         last_minus_h = keep.tile([P, S], F32)
         minus_h = [h_tiles[t + 1][:, S : 2 * S] for t in range(PACK - 1)] + [last_minus_h[:]]
         for t in range(PACK):
@@ -122,7 +120,7 @@ def tile_picked_codepagezquad_none_po_kernel(
 
         picked_bytes_2 = keep.tile([P, H], U8, tag="picked_bytes", align_bytes=64)
         nc.vector.tensor_copy(picked_bytes_2[:], d_scale_table[:].indirect(k2_list[:]))
-        place_scale_rows(placed_2, picked_bytes_2)
+        place_scale_rows(placed_1[:, S : S + H], picked_bytes_2)
 
         z_tiles = [
             keep.tile([P, hi - lo, PACK], BF16, name="z%d" % c, align_bytes=64) for c, (lo, hi) in enumerate(CHUNKS)
@@ -132,7 +130,10 @@ def tile_picked_codepagezquad_none_po_kernel(
 
         def fetch(t):
             tile = keep.tile([P, S], F32, name="fetched", tag="fetched%d" % t, align_bytes=64)
-            nc.vector.tensor_copy(tile[:], h_tiles[t][:].indirect(n2_list[:]))
+            step = S if t > 0 else S // 2
+            for lo in range(0, S, step):
+                entries = n2_list[:, lo // 16 : (lo + step) // 16]
+                nc.vector.tensor_copy(tile[:, lo : lo + step], h_tiles[t][:].indirect(entries))
             fetched.append(tile)
 
         fetch(0)
@@ -140,69 +141,75 @@ def tile_picked_codepagezquad_none_po_kernel(
             if t + 1 < PACK:
                 fetch(t + 1)
             nc.vector.tensor_tensor(
-                pages[t][:].indirect(n1_list[:]), fetched[t][:], minus_h[t], ALU.add
+                pages[t % 2][:].indirect(n1_list[:]), fetched[t][:], minus_h[t], ALU.add
             )
             if t == 0:
-                deal(w2_scales[:], placed_2[:], 16)
+                deal(w2_scales[:], placed_1[:, S : S + H], 16)
             minus_gs = keep.tile([P, 1], F32)
             nc.scalar.activation(minus_gs[:], gs_rows[:, t : t + 1], ACT.Copy, scale=-1.0)
             for c, (lo, hi) in enumerate(CHUNKS):
                 if (t, c) != (PACK - 1, len(CHUNKS) - 1):
                     nc.scalar.activation(
-                        z_tiles[c][:, :, t], pages[t][:, lo:hi], ACT.Copy, scale=minus_gs[:]
+                        z_tiles[c][:, :, t], pages[t % 2][:, lo:hi], ACT.Copy, scale=minus_gs[:]
                     )
 
         picked_words_2 = keep.tile([P, H], U32, tag="fetched%d" % (PACK - 1), align_bytes=64)
         nc.vector.tensor_copy(picked_words_2[:], d_word_table[:].bitcast(U32).indirect(k2_list[:]))
         w2_first = keep.tile([P, P], U32, align_bytes=64)
         deal(w2_first[:], picked_words_2[:], 4, 0, 1)
-        lo, hi = CHUNKS[-1]
-        nc.vector.tensor_scalar(
-            z_tiles[-1][:, :, PACK - 1], pages[PACK - 1][:, lo:hi], minus_gs[:], None, ALU.mult
-        )
+        z_codes = keep.tile([P, U], U32, align_bytes=64)
+        z_scales = zeroed_bytes(U, "z_scales")
 
-        z_codes, z_scales = {}, {}
-        z_scale_plane = zeroed_bytes(U, "z_scale_plane")
-        for c in (0, 2, 1):
+        def quantise_z(c):
             lo, hi = CHUNKS[c]
-            codes = keep.tile([P, hi - lo], U32, name="z_codes%d" % c, align_bytes=64)
-            scales = z_scale_plane[:, lo:hi]
-            nc.vector.quantize_mx(codes[:].bitcast(FP8X4), scales, z_tiles[c][:].rearrange("p w t -> p (w t)"))
-            z_codes.setdefault(c, codes)
-            z_scales.setdefault(c, scales)
-        w2_rest = keep.tile([P, H - P], U32, tag="z1", align_bytes=64)
+            nc.vector.quantize_mx(
+                z_codes[:, lo:hi].bitcast(FP8X4), z_scales[:, lo:hi], z_tiles[c][:].rearrange("p w t -> p (w t)")
+            )
+
+        quantise_z(0)
+        lo, hi = CHUNKS[3]
+        nc.vector.tensor_scalar(
+            z_tiles[3][:, :, PACK - 1], pages[(PACK - 1) % 2][:, lo:hi], minus_gs[:], None, ALU.mult
+        )
+        quantise_z(1)
+        quantise_z(3)
+        quantise_z(2)
+        w2_rest = keep.tile([P, H - P], U32, tag="z2", align_bytes=64)
         deal(w2_rest[:], picked_words_2[:], 4, 1, PACK)
         w2_codes = [w2_first[:]] + [w2_rest[:, t * P : (t + 1) * P] for t in range(PACK - 1)]
 
-        h2_tiles, h2_twins, h2_banks = [], [], []
+        def second_product(target, t, lo, hi):
+            nc.tensor.matmul_mx(
+                target,
+                lhsT=w2_codes[t].bitcast(FP8X4),
+                lhsT_scale=w2_scales[:, t * P : (t + 1) * P],
+                rhs=z_codes[:, lo:hi].bitcast(FP8X4),
+                rhs_scale=z_scales[:, lo:hi],
+                start=True,
+                stop=True,
+            )
+
+        h2_tiles = [keep.tile([P, U], F32, name="h2_%d" % t) for t in range(PACK)]
+        h2_twins = [keep.tile([P, U], F32, name="h2_twin%d" % t) for t in range(PACK)]
+        bank = psum.tile([P, BANK], F32, name="h2_bank", tag="bank0")
+        for lo, hi in CHUNKS[:2]:
+            second_product(bank[:, lo:hi], 0, lo, hi)
+        nc.scalar.activation(h2_tiles[0][:, 0:BANK], bank[:], ACT.Copy, scale=0.0625)
+        nc.scalar.activation(h2_twins[0][:, 0:BANK], bank[:], ACT.Copy, scale=0.0625)
+        for c, tag in ((3, "bank1"), (2, "bank7")):
+            lo, hi = CHUNKS[c]
+            bank = psum.tile([P, hi - lo], F32, name="h2_bank", tag=tag)
+            second_product(bank[:], 0, lo, hi)
+            nc.vector.tensor_scalar(h2_tiles[0][:, lo:hi], bank[:], 0.0625, None, ALU.mult)
+        for t in range(1, PACK):
+            for b in range(2):
+                columns = slice(b * BANK, (b + 1) * BANK)
+                bank = psum.tile([P, BANK], F32, name="h2_bank", tag="bank%d" % (2 * t + b))
+                second_product(bank[:], t, columns.start, columns.stop)
+                nc.scalar.activation(h2_tiles[t][:, columns], bank[:], ACT.Copy, scale=0.0625)
+            nc.scalar.copy(h2_twins[t][:, 0:BANK], h2_tiles[t][:, 0:BANK])
         for t in range(PACK):
-            banks = [psum.tile([P, BANK], F32, name="h2_bank", tag="bank%d" % (2 * t + b)) for b in range(2)]
-            rows = slice(t * P, (t + 1) * P)
-            for c in (0, 2, 1):
-                lo, hi = CHUNKS[c]
-                b = lo // BANK
-                nc.tensor.matmul_mx(
-                    banks[b][:, lo - b * BANK : hi - b * BANK],
-                    lhsT=w2_codes[t].bitcast(FP8X4),
-                    lhsT_scale=w2_scales[:, rows],
-                    rhs=z_codes[c][:].bitcast(FP8X4),
-                    rhs_scale=z_scales[c],
-                    start=True,
-                    stop=True,
-                )
-            h2 = keep.tile([P, U], F32, name="h2_%d" % t)
-            twin = keep.tile([P, U], F32, name="h2_twin%d" % t)
-            nc.scalar.activation(h2[:, 0:BANK], banks[0][:], ACT.Copy, scale=0.0625)
-            nc.scalar.activation(twin[:, 0:BANK], banks[0][:], ACT.Copy, scale=0.0625)
-            if t == 0:
-                nc.vector.tensor_scalar(h2[:, BANK:U], banks[1][:], 0.0625, None, ALU.mult)
-            else:
-                nc.scalar.activation(h2[:, BANK:U], banks[1][:], ACT.Copy, scale=0.0625)
-            h2_tiles.append(h2)
-            h2_twins.append(twin)
-            h2_banks.append(banks)
-        for t in range(PACK):
-            nc.scalar.activation(h2_twins[t][:, BANK:U], h2_banks[t][1][:], ACT.Copy, scale=0.0625)
+            nc.scalar.copy(h2_twins[t][:, BANK:U], h2_tiles[t][:, BANK:U])
 
         out_rows = out_0.rearrange("(p t) w -> p t w", t=PACK)
         out_words = out_1[0].rearrange("p n t -> p (n t)").bitcast(I32)

@@ -17,9 +17,17 @@ ACT = mybir.ActivationFunctionType
 
 P = 128
 PACK = 4
-QUADS = 4
-BANK = 512
-CHUNKS = ((0, 256), (256, 512), (512, 768), (768, 1024))
+LAST = PACK - 1
+BLOCKS = K // 32
+BLOCK_PARTITIONS = P // BLOCKS
+QUADRANT = 32
+PER_COLUMN = 16
+LINE = 16
+HALF = 512
+QUARTER = 256
+PAGES = 2
+PRODUCT_SCALE = 0.0625
+OUT_SCALE = 0.75
 
 
 def tile_picked_codepagezquad_none_po_kernel(
@@ -36,147 +44,145 @@ def tile_picked_codepagezquad_none_po_kernel(
             nc.sync.dma_start(tile[:], source)
             return tile
 
-        def zeroed_bytes(width, name):
+        def load_scale_rows(table, scales):
+            rows = scales[0].bitcast(I32)
+            repeated = rows.unsqueeze(1).to_broadcast([BLOCKS, BLOCK_PARTITIONS, rows.shape[1]])
+            nc.sync.dma_start(table[:].bitcast(I32), repeated)
+
+        def load_words(table, words):
+            nc.sync.dma_start(table[:], words[0].rearrange("p n t -> p (n t)").bitcast(I32))
+
+        def zeroed_plane(width, name):
             tile = keep.tile([P, width], U8, name=name, align_bytes=64)
             nc.vector.memset(tile[:].bitcast(I32), 0)
             return tile
 
-        def load_scale_rows(table, scales):
-            rows = scales[0].bitcast(I32)
-            nc.sync.dma_start(table[:].bitcast(I32), rows.unsqueeze(1).to_broadcast([16, 8, rows.shape[1]]))
+        def entries(index_list, lo, hi):
+            return index_list[:, lo // PER_COLUMN : hi // PER_COLUMN]
 
-        k1_list = load_list(k1, "k1_list")
-        d_scale_table = keep.tile([P, G], U8, align_bytes=64)
-        load_scale_rows(d_scale_table, d_scales)
         offs_list = load_list(offs, "offs_list")
         x_scale_table = keep.tile([P, T], U8, tag="x_scales_then_words", align_bytes=64)
         load_scale_rows(x_scale_table, x_scales)
+        k1_list = load_list(k1, "k1_list")
+        d_scale_table = keep.tile([P, G], U8, align_bytes=64)
+        load_scale_rows(d_scale_table, d_scales)
         x_word_table = keep.tile([P, T], I32)
-        nc.sync.dma_start(x_word_table[:], x_words[0].rearrange("p n t -> p (n t)").bitcast(I32))
+        load_words(x_word_table, x_words)
         n2_list = load_list(n2, "n2_list")
         n1_list = load_list(n1, "n1_list")
         k2_list = load_list(k2, "k2_list")
         d_word_table = keep.tile([P, G], I32)
-        nc.sync.dma_start(d_word_table[:], d_words[0].rearrange("p n t -> p (n t)").bitcast(I32))
+        load_words(d_word_table, d_words)
         n3_list = load_list(n3, "n3_list")
         n4_list = load_list(n4, "n4_list")
         gs_rows = keep.tile([P, PACK], F32)
         nc.sync.dma_start(gs_rows[:], gs.rearrange("(p t) one -> p (t one)", t=PACK))
 
-        placed_1 = zeroed_bytes(S + H, "placed_1")
-        pages = []
-        for t in range(2):
-            page = keep.tile([P, U], F32, name="page%d" % t)
-            (nc.vector if t == 0 else nc.gpsimd).memset(page[:], 0.0)
-            pages.append(page)
+        tokens = slice(0, S)
+        weights = slice(S, S + H)
+        placed_bytes = zeroed_plane(S + H, "placed_bytes")
 
+        pages = [keep.tile([P, U], F32, name="page%d" % i) for i in range(PAGES)]
+        nc.vector.memset(pages[0][:], 0.0)
+        nc.gpsimd.memset(pages[1][:], 0.0)
 
         def place_scale_rows(placed, picked):
-            for q in range(QUADS):
+            for q in range(P // QUADRANT):
+                base = QUADRANT * q
                 queue = nc.sync if q % 2 == 0 else nc.scalar
                 queue.dma_start(
-                    placed[32 * q : 32 * q + 4, :].bitcast(I32),
-                    picked[32 * q : 32 * q + 32 : 8, :].bitcast(I32),
+                    placed[base : base + PACK, :].bitcast(I32),
+                    picked[base : base + QUADRANT : BLOCK_PARTITIONS, :].bitcast(I32),
                 )
 
-        def deal(dealt, picked, run, first=0, last=PACK):
+        def deal(dealt, picked, run, first, last):
             nc.vector.tensor_copy(
                 dealt.rearrange("p (t c i) -> p c t i", t=last - first, i=run),
                 picked.rearrange("p (c i t) -> p c t i", t=PACK, i=run)[:, :, first:last, :],
             )
 
-        picked_bytes_1 = keep.tile([P, S + H], U8, tag="picked_bytes", align_bytes=64)
-        nc.vector.tensor_copy(picked_bytes_1[:, S : S + H], d_scale_table[:].indirect(k1_list[:]))
-        nc.vector.tensor_copy(picked_bytes_1[:, 0:S], x_scale_table[:].indirect(offs_list[:]))
-        place_scale_rows(placed_1, picked_bytes_1)
-        picked_words_1 = keep.tile([P, S + H], U32, tag="x_scales_then_words", align_bytes=64)
-        nc.vector.tensor_copy(picked_words_1[:, 0:S], x_word_table[:].bitcast(U32).indirect(offs_list[:]))
-        nc.vector.tensor_copy(picked_words_1[:, S : S + H], d_word_table[:].bitcast(U32).indirect(k1_list[:]))
-        w1_first = keep.tile([P, P], U32, align_bytes=64)
-        deal(w1_first[:], picked_words_1[:, S : S + H], 4, 0, 1)
-        w1_scales = keep.tile([P, H], U8, align_bytes=64)
-        deal(w1_scales[:], placed_1[:, S : S + H], 16)
-        w1_rest = keep.tile([P, H - P], U32, align_bytes=64)
-        deal(w1_rest[:], picked_words_1[:, S : S + H], 4, 1, PACK)
-        w1_codes = [w1_first[:]] + [w1_rest[:, t * P : (t + 1) * P] for t in range(PACK - 1)]
+        def row_tile_weights(first_codes, other_codes):
+            return [first_codes[:]] + [other_codes[:, t * P : (t + 1) * P] for t in range(LAST)]
 
-        h_tiles = [keep.tile([P, 2 * S if t > 0 else S], F32, name="h%d" % t) for t in range(PACK)]
+        picked_bytes_1 = keep.tile([P, S + H], U8, tag="bytes_1_then_words_2", align_bytes=64)
+        nc.vector.tensor_copy(picked_bytes_1[:, tokens], x_scale_table[:].indirect(offs_list[:]))
+        nc.vector.tensor_copy(picked_bytes_1[:, weights], d_scale_table[:].indirect(k1_list[:]))
+        place_scale_rows(placed_bytes, picked_bytes_1)
+        picked_words_1 = keep.tile([P, S + H], U32, tag="x_scales_then_words", align_bytes=64)
+        nc.vector.tensor_copy(picked_words_1[:, tokens], x_word_table[:].bitcast(U32).indirect(offs_list[:]))
+        nc.vector.tensor_copy(picked_words_1[:, weights], d_word_table[:].bitcast(U32).indirect(k1_list[:]))
+        w1_first = keep.tile([P, P], U32, align_bytes=64)
+        deal(w1_first[:], picked_words_1[:, weights], LINE // 4, 0, 1)
+        w1_scales = keep.tile([P, H], U8, align_bytes=64)
+        deal(w1_scales[:], placed_bytes[:, weights], LINE, 0, PACK)
+        w1_others = keep.tile([P, H - P], U32, align_bytes=64)
+        deal(w1_others[:], picked_words_1[:, weights], LINE // 4, 1, PACK)
+        w1_codes = row_tile_weights(w1_first, w1_others)
+
+        relu_h = [keep.tile([P, 2 * S if t > 0 else S], F32, name="relu_h%d" % t) for t in range(PACK)]
         last_minus_h = keep.tile([P, S], F32)
-        minus_h = [h_tiles[t + 1][:, S : 2 * S] for t in range(PACK - 1)] + [last_minus_h[:]]
+        minus_h = [relu_h[t + 1][:, S : 2 * S] for t in range(LAST)] + [last_minus_h[:]]
         for t in range(PACK):
-            bank = psum.tile([P, BANK], F32, name="h_bank", tag="bank%d" % (2 * t + 1))
-            rows = slice(t * P, (t + 1) * P)
+            h_bank = psum.tile([P, S], F32, tag="bank%d" % (2 * t + 1))
             nc.tensor.matmul_mx(
-                bank[:],
+                h_bank[:],
                 lhsT=w1_codes[t].bitcast(FP8X4),
-                lhsT_scale=w1_scales[:, rows],
-                rhs=picked_words_1[:, 0:S].bitcast(FP8X4),
-                rhs_scale=placed_1[:, 0:S],
+                lhsT_scale=w1_scales[:, t * P : (t + 1) * P],
+                rhs=picked_words_1[:, tokens].bitcast(FP8X4),
+                rhs_scale=placed_bytes[:, tokens],
                 start=True,
                 stop=True,
             )
-            nc.scalar.activation(h_tiles[t][:, 0:S], bank[:], ACT.Relu, scale=0.0625)
-            nc.scalar.activation(minus_h[t], bank[:], ACT.Copy, scale=-0.0625)
+            nc.scalar.activation(relu_h[t][:, 0:S], h_bank[:], ACT.Relu, scale=PRODUCT_SCALE)
+            nc.scalar.activation(minus_h[t], h_bank[:], ACT.Copy, scale=-PRODUCT_SCALE)
 
-        picked_bytes_2 = keep.tile([P, H], U8, tag="picked_bytes", align_bytes=64)
+        picked_bytes_2 = keep.tile([P, H], U8, align_bytes=64)
         nc.vector.tensor_copy(picked_bytes_2[:], d_scale_table[:].indirect(k2_list[:]))
-        place_scale_rows(placed_1[:, S : S + H], picked_bytes_2)
-
-        z_tiles = [
-            keep.tile([P, hi - lo, PACK], BF16, name="z%d" % c, align_bytes=64) for c, (lo, hi) in enumerate(CHUNKS)
-        ]
-        fetched = []
+        place_scale_rows(placed_bytes[:, weights], picked_bytes_2)
+        picked_words_2 = keep.tile([P, H], U32, tag="bytes_1_then_words_2", align_bytes=64)
+        nc.vector.tensor_copy(picked_words_2[:], d_word_table[:].bitcast(U32).indirect(k2_list[:]))
+        w2_first = keep.tile([P, P], U32, align_bytes=64)
+        deal(w2_first[:], picked_words_2[:], LINE // 4, 0, 1)
         w2_scales = keep.tile([P, H], U8, align_bytes=64)
 
+        quarters = [(lo, lo + QUARTER) for lo in range(0, U, QUARTER)]
+        z_quarters = [
+            keep.tile([P, QUARTER, PACK], BF16, name="z%d" % c, align_bytes=64) for c in range(len(quarters))
+        ]
+        fetched = [keep.tile([P, S], F32, name="fetched%d" % t) for t in range(PACK)]
+
         def fetch(t):
-            tile = keep.tile([P, S], F32, name="fetched", tag="fetched%d" % t, align_bytes=64)
             step = S if t > 0 else S // 2
             for lo in range(0, S, step):
-                entries = n2_list[:, lo // 16 : (lo + step) // 16]
-                nc.vector.tensor_copy(tile[:, lo : lo + step], h_tiles[t][:].indirect(entries))
-            fetched.append(tile)
+                window = relu_h[t][:].indirect(entries(n2_list, lo, lo + step))
+                nc.vector.tensor_copy(fetched[t][:, lo : lo + step], window)
 
         fetch(0)
         for t in range(PACK):
-            if t + 1 < PACK:
+            page = pages[t % PAGES]
+            if t < LAST:
                 fetch(t + 1)
-            nc.vector.tensor_tensor(
-                pages[t % 2][:].indirect(n1_list[:]), fetched[t][:], minus_h[t], ALU.add
-            )
+            nc.vector.tensor_tensor(page[:].indirect(n1_list[:]), fetched[t][:], minus_h[t], ALU.add)
             if t == 0:
-                deal(w2_scales[:], placed_1[:, S : S + H], 16)
+                deal(w2_scales[:], placed_bytes[:, weights], LINE, 0, PACK)
             minus_gs = keep.tile([P, 1], F32)
             nc.scalar.activation(minus_gs[:], gs_rows[:, t : t + 1], ACT.Copy, scale=-1.0)
-            for c, (lo, hi) in enumerate(CHUNKS):
-                if (t, c) != (PACK - 1, len(CHUNKS) - 1):
-                    nc.scalar.activation(
-                        z_tiles[c][:, :, t], pages[t % 2][:, lo:hi], ACT.Copy, scale=minus_gs[:]
-                    )
+            for c, (lo, hi) in enumerate(quarters):
+                if t == LAST and lo < HALF:
+                    nc.vector.tensor_scalar(z_quarters[c][:, :, t], page[:, lo:hi], minus_gs[:], None, ALU.mult)
+                else:
+                    nc.scalar.activation(z_quarters[c][:, :, t], page[:, lo:hi], ACT.Copy, scale=minus_gs[:])
 
-        picked_words_2 = keep.tile([P, H], U32, tag="fetched%d" % (PACK - 1), align_bytes=64)
-        nc.vector.tensor_copy(picked_words_2[:], d_word_table[:].bitcast(U32).indirect(k2_list[:]))
-        w2_first = keep.tile([P, P], U32, align_bytes=64)
-        deal(w2_first[:], picked_words_2[:], 4, 0, 1)
         z_codes = keep.tile([P, U], U32, align_bytes=64)
-        z_scales = zeroed_bytes(U, "z_scales")
-
-        def quantise_z(c):
-            lo, hi = CHUNKS[c]
+        z_scales = zeroed_plane(U, "z_scales")
+        for c, (lo, hi) in enumerate(quarters):
             nc.vector.quantize_mx(
-                z_codes[:, lo:hi].bitcast(FP8X4), z_scales[:, lo:hi], z_tiles[c][:].rearrange("p w t -> p (w t)")
+                z_codes[:, lo:hi].bitcast(FP8X4), z_scales[:, lo:hi], z_quarters[c][:].rearrange("p w t -> p (w t)")
             )
 
-        quantise_z(0)
-        lo, hi = CHUNKS[3]
-        nc.vector.tensor_scalar(
-            z_tiles[3][:, :, PACK - 1], pages[(PACK - 1) % 2][:, lo:hi], minus_gs[:], None, ALU.mult
-        )
-        quantise_z(1)
-        quantise_z(3)
-        quantise_z(2)
-        w2_rest = keep.tile([P, H - P], U32, tag="z2", align_bytes=64)
-        deal(w2_rest[:], picked_words_2[:], 4, 1, PACK)
-        w2_codes = [w2_first[:]] + [w2_rest[:, t * P : (t + 1) * P] for t in range(PACK - 1)]
+        w2_others = keep.tile([P, H - P], U32, tag="z%d" % (len(quarters) - 1), align_bytes=64)
+        deal(w2_others[:], picked_words_2[:], LINE // 4, 1, PACK)
+        w2_codes = row_tile_weights(w2_first, w2_others)
 
         def second_product(target, t, lo, hi):
             nc.tensor.matmul_mx(
@@ -189,58 +195,60 @@ def tile_picked_codepagezquad_none_po_kernel(
                 stop=True,
             )
 
-        h2_tiles = [keep.tile([P, U], F32, name="h2_%d" % t) for t in range(PACK)]
-        h2_twins = [keep.tile([P, U], F32, name="h2_twin%d" % t) for t in range(PACK)]
-        bank = psum.tile([P, BANK], F32, name="h2_bank", tag="bank0")
-        for lo, hi in CHUNKS[:2]:
-            second_product(bank[:, lo:hi], 0, lo, hi)
-        nc.scalar.activation(h2_tiles[0][:, 0:BANK], bank[:], ACT.Copy, scale=0.0625)
-        nc.scalar.activation(h2_twins[0][:, 0:BANK], bank[:], ACT.Copy, scale=0.0625)
-        for c, tag in ((3, "bank1"), (2, "bank7")):
-            lo, hi = CHUNKS[c]
-            bank = psum.tile([P, hi - lo], F32, name="h2_bank", tag=tag)
-            second_product(bank[:], 0, lo, hi)
-            nc.vector.tensor_scalar(h2_tiles[0][:, lo:hi], bank[:], 0.0625, None, ALU.mult)
+        h2_windows = [keep.tile([P, U], F32, name="h2_window%d" % t) for t in range(PACK)]
+        h2_plain = [keep.tile([P, U], F32, name="h2_plain%d" % t) for t in range(PACK)]
+
+        first_bank = psum.tile([P, HALF], F32, tag="bank0")
+        for lo, hi in quarters[:2]:
+            second_product(first_bank[:, lo:hi], 0, lo, hi)
+        nc.scalar.activation(h2_windows[0][:, 0:HALF], first_bank[:], ACT.Copy, scale=PRODUCT_SCALE)
+        nc.scalar.activation(h2_plain[0][:, 0:HALF], first_bank[:], ACT.Copy, scale=PRODUCT_SCALE)
+        for (lo, hi), bank_tag in zip(quarters[2:], ("bank1", "bank%d" % (2 * LAST + 1))):
+            quarter_bank = psum.tile([P, QUARTER], F32, tag=bank_tag)
+            second_product(quarter_bank[:], 0, lo, hi)
+            nc.vector.tensor_scalar(h2_windows[0][:, lo:hi], quarter_bank[:], PRODUCT_SCALE, None, ALU.mult)
         for t in range(1, PACK):
-            for b in range(2):
-                columns = slice(b * BANK, (b + 1) * BANK)
-                bank = psum.tile([P, BANK], F32, name="h2_bank", tag="bank%d" % (2 * t + b))
-                second_product(bank[:], t, columns.start, columns.stop)
-                nc.scalar.activation(h2_tiles[t][:, columns], bank[:], ACT.Copy, scale=0.0625)
-            nc.scalar.copy(h2_twins[t][:, 0:BANK], h2_tiles[t][:, 0:BANK])
+            for half in range(2):
+                lo, hi = half * HALF, (half + 1) * HALF
+                h2_bank = psum.tile([P, HALF], F32, tag="bank%d" % (2 * t + half))
+                second_product(h2_bank[:], t, lo, hi)
+                nc.scalar.activation(h2_windows[t][:, lo:hi], h2_bank[:], ACT.Copy, scale=PRODUCT_SCALE)
+            nc.scalar.copy(h2_plain[t][:, 0:HALF], h2_windows[t][:, 0:HALF])
         for t in range(PACK):
-            nc.scalar.copy(h2_twins[t][:, BANK:U], h2_tiles[t][:, BANK:U])
+            nc.scalar.copy(h2_plain[t][:, HALF:U], h2_windows[t][:, HALF:U])
 
         out_rows = out_0.rearrange("(p t) w -> p t w", t=PACK)
         out_words = out_1[0].rearrange("p n t -> p (n t)").bitcast(I32)
-        out_scales = keep.tile([P, U], U8, align_bytes=64)
-        diff_3 = keep.tile([P, 2, PACK, BANK], F32)
-        diff_4 = keep.tile([P, 2, PACK, BANK], F32)
-        result = keep.tile([P, 2, PACK, BANK], F32)
+        diff_3 = keep.tile([P, 2, PACK, HALF], F32)
+        diff_4 = keep.tile([P, 2, PACK, HALF], F32)
+        result = keep.tile([P, 2, PACK, HALF], F32)
         rounded = keep.tile([P, U, PACK], BF16, align_bytes=64)
         out_codes = keep.tile([P, U], I32, align_bytes=64)
+        out_scales = keep.tile([P, U], U8, align_bytes=64)
+
+        def part(tile, first, last, lo, hi):
+            return tile[:, lo // HALF, first:last, lo % HALF : lo % HALF + hi - lo]
 
         def differ(diff, index_list, t, lo, hi):
             nc.vector.tensor_tensor(
-                diff[:, lo // BANK, t, lo % BANK : lo % BANK + hi - lo],
-                h2_tiles[t][:].indirect(index_list[:, lo // 16 : hi // 16]),
-                h2_twins[t][:, lo:hi],
+                part(diff, t, t + 1, lo, hi).rearrange("p t w -> p (t w)"),
+                h2_windows[t][:].indirect(entries(index_list, lo, hi)),
+                h2_plain[t][:, lo:hi],
                 ALU.subtract,
             )
 
-        def finish(first, last, lo, hi):
-            views = [
-                tile[:, lo // BANK, first:last, lo % BANK : lo % BANK + hi - lo] for tile in (result, diff_3, diff_4)
-            ]
-            nc.vector.scalar_tensor_tensor(views[0], views[1], 0.75, views[2], ALU.mult, ALU.mult)
-            nc.sync.dma_start(out_rows[:, first:last, lo:hi], views[0])
-            nc.scalar.activation(
-                rounded[:, lo:hi, first:last].rearrange("p (c i) t -> p c t i", i=4),
-                views[0].rearrange("p t (c i) -> p c t i", i=4),
-                ACT.Copy,
+        def multiply(first, last, lo, hi):
+            product, left, right = [part(tile, first, last, lo, hi) for tile in (result, diff_3, diff_4)]
+            nc.vector.scalar_tensor_tensor(product, left, OUT_SCALE, right, ALU.mult, ALU.mult)
+            nc.sync.dma_start(out_rows[:, first:last, lo:hi], product)
+
+        def round_result(copy, first, last, lo, hi):
+            copy(
+                rounded[:, lo:hi, first:last].rearrange("p (c i) t -> p c t i", i=LINE // 4),
+                part(result, first, last, lo, hi).rearrange("p t (c i) -> p c t i", i=LINE // 4),
             )
 
-        def quantise(lo, hi):
+        def quantise_result(lo, hi):
             nc.vector.quantize_mx(
                 out_codes[:, lo:hi].bitcast(FP8X4),
                 out_scales[:, lo:hi],
@@ -248,27 +256,35 @@ def tile_picked_codepagezquad_none_po_kernel(
             )
             nc.sync.dma_start(out_words[:, lo:hi], out_codes[:, lo:hi])
 
-        last = PACK - 1
-        mid = BANK + BANK // 2
         for t in range(PACK):
-            differ(diff_3, n3_list, t, 0, BANK)
-            differ(diff_4, n4_list, t, 0, BANK)
-        differ(diff_3, n3_list, 0, BANK, U)
-        finish(0, PACK, 0, BANK)
-        differ(diff_4, n4_list, 0, BANK, U)
-        for t in range(1, last):
-            differ(diff_3, n3_list, t, BANK, U)
-            differ(diff_4, n4_list, t, BANK, U)
-        quantise(0, BANK)
-        differ(diff_3, n3_list, last, BANK, mid)
-        finish(0, last, BANK, U)
-        differ(diff_4, n4_list, last, BANK, mid)
-        differ(diff_3, n3_list, last, mid, U)
-        finish(last, PACK, BANK, mid)
-        differ(diff_4, n4_list, last, mid, U)
-        finish(last, PACK, mid, U)
-        quantise(BANK, mid)
-        quantise(mid, U)
-        for q in range(QUADS):
+            differ(diff_3, n3_list, t, 0, HALF)
+            differ(diff_4, n4_list, t, 0, HALF)
+        differ(diff_3, n3_list, 0, HALF, U)
+        multiply(0, PACK, 0, HALF)
+        round_result(nc.scalar.copy, 0, PACK, 0, HALF)
+
+        cut = U - QUARTER
+        differ(diff_4, n4_list, 0, HALF, U)
+        for t in range(1, LAST):
+            differ(diff_3, n3_list, t, HALF, U)
+            differ(diff_4, n4_list, t, HALF, U)
+        quantise_result(0, HALF)
+        differ(diff_3, n3_list, LAST, HALF, cut)
+        multiply(0, LAST, HALF, U)
+        round_result(nc.scalar.copy, 0, LAST, HALF, cut)
+        differ(diff_4, n4_list, LAST, HALF, cut)
+        differ(diff_3, n3_list, LAST, cut, U)
+        multiply(LAST, PACK, HALF, cut)
+        round_result(nc.scalar.copy, LAST, PACK, HALF, cut)
+        round_result(nc.scalar.copy, 0, LAST - 1, cut, U)
+        differ(diff_4, n4_list, LAST, cut, U)
+        multiply(LAST, PACK, cut, U)
+        quantise_result(HALF, cut)
+        round_result(nc.vector.tensor_copy, LAST - 1, PACK, cut, U)
+        quantise_result(cut, U)
+        for q in range(P // QUADRANT):
             queue = nc.scalar if q % 2 == 0 else nc.sync
-            queue.dma_start(out_2[0, 4 * q : 4 * q + 4, :].bitcast(I32), out_scales[32 * q : 32 * q + 4, :].bitcast(I32))
+            queue.dma_start(
+                out_2[0, PACK * q : PACK * (q + 1), :].bitcast(I32),
+                out_scales[QUADRANT * q : QUADRANT * q + PACK, :].bitcast(I32),
+            )

from contextlib import ExitStack

import concourse.mybir as mybir

K, T, S, G, H, U = 512, 1024, 512, 2048, 512, 1024
FLOPS = 2 * K * H * S + 2 * K * H * U

F32 = mybir.dt.float32
BF16 = mybir.dt.bfloat16
I32 = mybir.dt.int32
U32 = mybir.dt.uint32
U16 = mybir.dt.uint16
U8 = mybir.dt.uint8
FP8X4 = mybir.dt.float8_e4m3fn_x4
ALU = mybir.AluOpType
ACT = mybir.ActivationFunctionType

P = 128
PACK = 4
LAST = PACK - 1
BLOCKS = K // 32
BLOCK_PARTITIONS = P // BLOCKS
QUADRANT = 32
PER_COLUMN = 16
LINE = 16
HALF = 512
QUARTER = 256
PAGES = 2
PRODUCT_SCALE = 0.0625
OUT_SCALE = 0.75


def tile_picked_codepagezquad_none_po_kernel(
    tc, x_words, x_scales, d_words, d_scales, gs, offs, k1, n1, n2, k2, n3, n4, out_0, out_1, out_2
):
    nc = tc.nc
    with ExitStack() as ctx:
        lists = ctx.enter_context(tc.tile_pool(name="lists", bufs=1))
        keep = ctx.enter_context(tc.tile_pool(name="keep", bufs=1))
        psum = ctx.enter_context(tc.psum_pool(name="psum", bufs=1))

        def load_list(source, name):
            tile = lists.tile(list(source.shape), U16, name=name)
            nc.sync.dma_start(tile[:], source)
            return tile

        def load_scale_rows(table, scales):
            rows = scales[0].bitcast(I32)
            repeated = rows.unsqueeze(1).to_broadcast([BLOCKS, BLOCK_PARTITIONS, rows.shape[1]])
            nc.sync.dma_start(table[:].bitcast(I32), repeated)

        def load_words(table, words):
            nc.sync.dma_start(table[:], words[0].rearrange("p n t -> p (n t)").bitcast(I32))

        def zeroed_plane(width, name):
            tile = keep.tile([P, width], U8, name=name, align_bytes=64)
            nc.vector.memset(tile[:].bitcast(I32), 0)
            return tile

        def entries(index_list, lo, hi):
            return index_list[:, lo // PER_COLUMN : hi // PER_COLUMN]

        offs_list = load_list(offs, "offs_list")
        x_scale_table = keep.tile([P, T], U8, tag="x_scales_then_words", align_bytes=64)
        load_scale_rows(x_scale_table, x_scales)
        k1_list = load_list(k1, "k1_list")
        d_scale_table = keep.tile([P, G], U8, align_bytes=64)
        load_scale_rows(d_scale_table, d_scales)
        x_word_table = keep.tile([P, T], I32)
        load_words(x_word_table, x_words)
        n2_list = load_list(n2, "n2_list")
        n1_list = load_list(n1, "n1_list")
        k2_list = load_list(k2, "k2_list")
        d_word_table = keep.tile([P, G], I32)
        load_words(d_word_table, d_words)
        n3_list = load_list(n3, "n3_list")
        n4_list = load_list(n4, "n4_list")
        gs_rows = keep.tile([P, PACK], F32)
        nc.sync.dma_start(gs_rows[:], gs.rearrange("(p t) one -> p (t one)", t=PACK))

        tokens = slice(0, S)
        weights = slice(S, S + H)
        placed_bytes = zeroed_plane(S + H, "placed_bytes")

        pages = [keep.tile([P, U], F32, name="page%d" % i) for i in range(PAGES)]
        nc.vector.memset(pages[0][:], 0.0)
        nc.gpsimd.memset(pages[1][:], 0.0)

        def place_scale_rows(placed, picked):
            for q in range(P // QUADRANT):
                base = QUADRANT * q
                queue = nc.sync if q % 2 == 0 else nc.scalar
                queue.dma_start(
                    placed[base : base + PACK, :].bitcast(I32),
                    picked[base : base + QUADRANT : BLOCK_PARTITIONS, :].bitcast(I32),
                )

        def deal(dealt, picked, run, first, last):
            nc.vector.tensor_copy(
                dealt.rearrange("p (t c i) -> p c t i", t=last - first, i=run),
                picked.rearrange("p (c i t) -> p c t i", t=PACK, i=run)[:, :, first:last, :],
            )

        def row_tile_weights(first_codes, other_codes):
            return [first_codes[:]] + [other_codes[:, t * P : (t + 1) * P] for t in range(LAST)]

        picked_bytes_1 = keep.tile([P, S + H], U8, tag="bytes_1_then_words_2", align_bytes=64)
        nc.vector.tensor_copy(picked_bytes_1[:, tokens], x_scale_table[:].indirect(offs_list[:]))
        nc.vector.tensor_copy(picked_bytes_1[:, weights], d_scale_table[:].indirect(k1_list[:]))
        place_scale_rows(placed_bytes, picked_bytes_1)
        picked_words_1 = keep.tile([P, S + H], U32, tag="x_scales_then_words", align_bytes=64)
        nc.vector.tensor_copy(picked_words_1[:, tokens], x_word_table[:].bitcast(U32).indirect(offs_list[:]))
        nc.vector.tensor_copy(picked_words_1[:, weights], d_word_table[:].bitcast(U32).indirect(k1_list[:]))
        w1_first = keep.tile([P, P], U32, align_bytes=64)
        deal(w1_first[:], picked_words_1[:, weights], LINE // 4, 0, 1)
        w1_scales = keep.tile([P, H], U8, align_bytes=64)
        deal(w1_scales[:], placed_bytes[:, weights], LINE, 0, PACK)
        w1_others = keep.tile([P, H - P], U32, align_bytes=64)
        deal(w1_others[:], picked_words_1[:, weights], LINE // 4, 1, PACK)
        w1_codes = row_tile_weights(w1_first, w1_others)

        relu_h = [keep.tile([P, 2 * S if t > 0 else S], F32, name="relu_h%d" % t) for t in range(PACK)]
        last_minus_h = keep.tile([P, S], F32)
        minus_h = [relu_h[t + 1][:, S : 2 * S] for t in range(LAST)] + [last_minus_h[:]]
        for t in range(PACK):
            h_bank = psum.tile([P, S], F32, tag="bank%d" % (2 * t + 1))
            nc.tensor.matmul_mx(
                h_bank[:],
                lhsT=w1_codes[t].bitcast(FP8X4),
                lhsT_scale=w1_scales[:, t * P : (t + 1) * P],
                rhs=picked_words_1[:, tokens].bitcast(FP8X4),
                rhs_scale=placed_bytes[:, tokens],
                start=True,
                stop=True,
            )
            nc.scalar.activation(relu_h[t][:, 0:S], h_bank[:], ACT.Relu, scale=PRODUCT_SCALE)
            nc.scalar.activation(minus_h[t], h_bank[:], ACT.Copy, scale=-PRODUCT_SCALE)

        picked_bytes_2 = keep.tile([P, H], U8, align_bytes=64)
        nc.vector.tensor_copy(picked_bytes_2[:], d_scale_table[:].indirect(k2_list[:]))
        place_scale_rows(placed_bytes[:, weights], picked_bytes_2)
        picked_words_2 = keep.tile([P, H], U32, tag="bytes_1_then_words_2", align_bytes=64)
        nc.vector.tensor_copy(picked_words_2[:], d_word_table[:].bitcast(U32).indirect(k2_list[:]))
        w2_first = keep.tile([P, P], U32, align_bytes=64)
        deal(w2_first[:], picked_words_2[:], LINE // 4, 0, 1)
        w2_scales = keep.tile([P, H], U8, align_bytes=64)

        quarters = [(lo, lo + QUARTER) for lo in range(0, U, QUARTER)]
        z_quarters = [
            keep.tile([P, QUARTER, PACK], BF16, name="z%d" % c, align_bytes=64) for c in range(len(quarters))
        ]
        fetched = [keep.tile([P, S], F32, name="fetched%d" % t) for t in range(PACK)]

        def fetch(t):
            step = S if t > 0 else S // 2
            for lo in range(0, S, step):
                window = relu_h[t][:].indirect(entries(n2_list, lo, lo + step))
                nc.vector.tensor_copy(fetched[t][:, lo : lo + step], window)

        fetch(0)
        for t in range(PACK):
            page = pages[t % PAGES]
            if t < LAST:
                fetch(t + 1)
            nc.vector.tensor_tensor(page[:].indirect(n1_list[:]), fetched[t][:], minus_h[t], ALU.add)
            if t == 0:
                deal(w2_scales[:], placed_bytes[:, weights], LINE, 0, PACK)
            minus_gs = keep.tile([P, 1], F32)
            nc.scalar.activation(minus_gs[:], gs_rows[:, t : t + 1], ACT.Copy, scale=-1.0)
            for c, (lo, hi) in enumerate(quarters):
                if t == LAST and lo < HALF:
                    nc.vector.tensor_scalar(z_quarters[c][:, :, t], page[:, lo:hi], minus_gs[:], None, ALU.mult)
                else:
                    nc.scalar.activation(z_quarters[c][:, :, t], page[:, lo:hi], ACT.Copy, scale=minus_gs[:])

        z_codes = keep.tile([P, U], U32, align_bytes=64)
        z_scales = zeroed_plane(U, "z_scales")
        for c, (lo, hi) in enumerate(quarters):
            nc.vector.quantize_mx(
                z_codes[:, lo:hi].bitcast(FP8X4), z_scales[:, lo:hi], z_quarters[c][:].rearrange("p w t -> p (w t)")
            )

        w2_others = keep.tile([P, H - P], U32, tag="z%d" % (len(quarters) - 1), align_bytes=64)
        deal(w2_others[:], picked_words_2[:], LINE // 4, 1, PACK)
        w2_codes = row_tile_weights(w2_first, w2_others)

        def second_product(target, t, lo, hi):
            nc.tensor.matmul_mx(
                target,
                lhsT=w2_codes[t].bitcast(FP8X4),
                lhsT_scale=w2_scales[:, t * P : (t + 1) * P],
                rhs=z_codes[:, lo:hi].bitcast(FP8X4),
                rhs_scale=z_scales[:, lo:hi],
                start=True,
                stop=True,
            )

        h2_windows = [keep.tile([P, U], F32, name="h2_window%d" % t) for t in range(PACK)]
        h2_plain = [keep.tile([P, U], F32, name="h2_plain%d" % t) for t in range(PACK)]

        first_bank = psum.tile([P, HALF], F32, tag="bank0")
        for lo, hi in quarters[:2]:
            second_product(first_bank[:, lo:hi], 0, lo, hi)
        nc.scalar.activation(h2_windows[0][:, 0:HALF], first_bank[:], ACT.Copy, scale=PRODUCT_SCALE)
        nc.scalar.activation(h2_plain[0][:, 0:HALF], first_bank[:], ACT.Copy, scale=PRODUCT_SCALE)
        for (lo, hi), bank_tag in zip(quarters[2:], ("bank1", "bank%d" % (2 * LAST + 1))):
            quarter_bank = psum.tile([P, QUARTER], F32, tag=bank_tag)
            second_product(quarter_bank[:], 0, lo, hi)
            nc.vector.tensor_scalar(h2_windows[0][:, lo:hi], quarter_bank[:], PRODUCT_SCALE, None, ALU.mult)
        for t in range(1, PACK):
            for half in range(2):
                lo, hi = half * HALF, (half + 1) * HALF
                h2_bank = psum.tile([P, HALF], F32, tag="bank%d" % (2 * t + half))
                second_product(h2_bank[:], t, lo, hi)
                nc.scalar.activation(h2_windows[t][:, lo:hi], h2_bank[:], ACT.Copy, scale=PRODUCT_SCALE)
            nc.scalar.copy(h2_plain[t][:, 0:HALF], h2_windows[t][:, 0:HALF])
        for t in range(PACK):
            nc.scalar.copy(h2_plain[t][:, HALF:U], h2_windows[t][:, HALF:U])

        out_rows = out_0.rearrange("(p t) w -> p t w", t=PACK)
        out_words = out_1[0].rearrange("p n t -> p (n t)").bitcast(I32)
        diff_3 = keep.tile([P, 2, PACK, HALF], F32)
        diff_4 = keep.tile([P, 2, PACK, HALF], F32)
        result = keep.tile([P, 2, PACK, HALF], F32)
        rounded = keep.tile([P, U, PACK], BF16, align_bytes=64)
        out_codes = keep.tile([P, U], I32, align_bytes=64)
        out_scales = keep.tile([P, U], U8, align_bytes=64)

        def part(tile, first, last, lo, hi):
            return tile[:, lo // HALF, first:last, lo % HALF : lo % HALF + hi - lo]

        def differ(diff, index_list, t, lo, hi):
            nc.vector.tensor_tensor(
                part(diff, t, t + 1, lo, hi).rearrange("p t w -> p (t w)"),
                h2_windows[t][:].indirect(entries(index_list, lo, hi)),
                h2_plain[t][:, lo:hi],
                ALU.subtract,
            )

        def multiply(first, last, lo, hi):
            product, left, right = [part(tile, first, last, lo, hi) for tile in (result, diff_3, diff_4)]
            nc.vector.scalar_tensor_tensor(product, left, OUT_SCALE, right, ALU.mult, ALU.mult)
            nc.sync.dma_start(out_rows[:, first:last, lo:hi], product)

        def round_result(copy, first, last, lo, hi):
            copy(
                rounded[:, lo:hi, first:last].rearrange("p (c i) t -> p c t i", i=LINE // 4),
                part(result, first, last, lo, hi).rearrange("p t (c i) -> p c t i", i=LINE // 4),
            )

        def quantise_result(lo, hi):
            nc.vector.quantize_mx(
                out_codes[:, lo:hi].bitcast(FP8X4),
                out_scales[:, lo:hi],
                rounded[:, lo:hi, :].rearrange("p w t -> p (w t)"),
            )
            nc.sync.dma_start(out_words[:, lo:hi], out_codes[:, lo:hi])

        for t in range(PACK):
            differ(diff_3, n3_list, t, 0, HALF)
            differ(diff_4, n4_list, t, 0, HALF)
        differ(diff_3, n3_list, 0, HALF, U)
        multiply(0, PACK, 0, HALF)
        round_result(nc.scalar.copy, 0, PACK, 0, HALF)

        cut = U - QUARTER
        differ(diff_4, n4_list, 0, HALF, U)
        for t in range(1, LAST):
            differ(diff_3, n3_list, t, HALF, U)
            differ(diff_4, n4_list, t, HALF, U)
        quantise_result(0, HALF)
        differ(diff_3, n3_list, LAST, HALF, cut)
        multiply(0, LAST, HALF, U)
        round_result(nc.scalar.copy, 0, LAST, HALF, cut)
        differ(diff_4, n4_list, LAST, HALF, cut)
        differ(diff_3, n3_list, LAST, cut, U)
        multiply(LAST, PACK, HALF, cut)
        round_result(nc.scalar.copy, LAST, PACK, HALF, cut)
        round_result(nc.scalar.copy, 0, LAST - 1, cut, U)
        differ(diff_4, n4_list, LAST, cut, U)
        multiply(LAST, PACK, cut, U)
        quantise_result(HALF, cut)
        round_result(nc.vector.tensor_copy, LAST - 1, PACK, cut, U)
        quantise_result(cut, U)
        for q in range(P // QUADRANT):
            queue = nc.scalar if q % 2 == 0 else nc.sync
            queue.dma_start(
                out_2[0, PACK * q : PACK * (q + 1), :].bitcast(I32),
                out_scales[QUADRANT * q : QUADRANT * q + PACK, :].bitcast(I32),
            )
